import numpy as np
import ml_dtypes


def mxq(x, axis, fmt="e4m3"):
    dtype, down = {"e4m3": (ml_dtypes.float8_e4m3fn, 7), "e5m2": (ml_dtypes.float8_e5m2, 14)}[fmt]
    v = np.moveaxis(np.asarray(x, np.float32).astype(ml_dtypes.bfloat16).astype(np.float64), axis, -1)
    blocks = v.reshape(v.shape[:-1] + (-1, 32))
    amax = np.abs(blocks).max(-1, keepdims=True)
    byte = np.maximum(np.where(amax > 0, np.frexp(amax)[1] - 1 + 127, 0) - down, 1)
    scale = np.exp2(byte - 127.0)
    codes = (blocks / scale).astype(np.float32).astype(dtype).astype(np.float64)
    return np.moveaxis((codes * scale).reshape(v.shape), -1, axis)


WIDE = False


def mx_kscale(k):
    if not WIDE:
        return np.ones(k)
    levels = np.array([10, -10, 5, -5, 0])
    if k % 512:
        return np.exp2(np.random.permutation(np.resize(levels, k // 32))).repeat(32)
    a = np.empty((k // 512, 16))
    for p in range(k // 512):
        a[p, :8] = np.random.permutation(np.resize(levels, 8))
        for g in range(8):
            far = levels[np.abs(levels - a[p, g]) >= 10]
            a[p, g + 8] = far[np.random.randint(len(far))]
    return np.exp2(a.ravel()).repeat(32)


def f64(x):
    return np.asarray(x).astype(np.float64)


def striped(idx):
    return np.tile(np.asarray(idx).reshape(-1, 16).T, (8, 1)).astype(np.uint16)


def unstriped(offs):
    return offs[:16].T.reshape(-1).astype(np.int64)


E2M1 = np.array([0.0, 0.5, 1.0, 1.5, 2.0, 3.0, 4.0, 6.0, -0.0, -0.5, -1.0, -1.5, -2.0, -3.0, -4.0, -6.0])


def pack_weight(w, fmt):
    k, n = w.shape
    w = f64(np.asarray(w, np.float32).astype(ml_dtypes.bfloat16)).reshape(k // 32, 32, n)
    amax = np.abs(w).max(1)
    if fmt == "e4m3":
        byte = np.frexp(amax)[1] - 1 + 127 - 7
    else:
        mant, ex = np.frexp(amax / 6.0)
        byte = np.where(mant > 0.5, ex, ex - 1) + 127
    byte = np.clip(np.where(amax > 0, byte, 1), 1, 254)
    scaled = (w * np.exp2(127.0 - byte)[:, None, :]).reshape(k, n).astype(np.float32)
    by_word = np.ascontiguousarray(scaled.reshape(k // 512, 128, 4, n).transpose(0, 1, 3, 2))
    if fmt == "e4m3":
        words = by_word.astype(ml_dtypes.float8_e4m3fn).view(np.uint8)
    else:
        c = by_word.astype(ml_dtypes.float4_e2m1fn).view(np.uint8) & 0xF
        words = (c[..., 0::2] | (c[..., 1::2] << 4)).reshape(k // 512, 128, 2 * n)
    return np.ascontiguousarray(words), np.ascontiguousarray(byte.astype(np.uint8).reshape(k // 512, 16, n))


def unpack_weight(words, scales, fmt):
    g, _, n = scales.shape
    words = np.ascontiguousarray(words).reshape(g, 128, n, -1)
    if fmt == "e4m3":
        vals = words.view(ml_dtypes.float8_e4m3fn).astype(np.float64)
    else:
        nib = np.empty((g, 128, n, 4), np.uint8)
        nib[..., 0::2] = words & 0xF
        nib[..., 1::2] = words >> 4
        vals = E2M1[nib]
    vals = vals * np.repeat(np.exp2(scales.astype(np.float64) - 127.0), 8, axis=1)[..., None]
    return vals.transpose(0, 1, 3, 2).reshape(g * 512, n)


B, N, T, D, NQ = 1, 512, 2048, 1024, 128


def setup_inputs():
    n = np.random.standard_normal
    idx = np.random.permutation(T)[:B * N]
    s = mx_kscale(D)[:, None]
    mid = n((D, T))
    kp = pack_weight((mid + np.abs(n((D, T)))) / s, "e2m1")
    cp = pack_weight((mid - np.abs(n((D, T)))) / s, "e2m1")
    return {
        "qT": (n((B, D, NQ)) * s * (1.00 / np.sqrt(D))).astype(np.float32),
        "k_words": np.ascontiguousarray(kp[0].reshape(1, 2, 128, T, 2).transpose(0, 2, 3, 1, 4)).reshape(1, 128, T, 4),
        "k_scales": kp[1],
        "c_words": np.ascontiguousarray(cp[0].reshape(1, 2, 128, T, 2).transpose(0, 2, 3, 1, 4)).reshape(1, 128, T, 4),
        "c_scales": cp[1],
        "th": (n((B, NQ, 1))).astype(np.float32),
        "offs": striped(idx),
    }


def reference(qT, k_words, k_scales, c_words, c_scales, th, offs):
    idx = unstriped(offs)
    pick = lambda x, which: x[:, which].reshape(x.shape[0], B, -1).transpose(1, 0, 2)
    k = unpack_weight(k_words.reshape(1, 128, T, 2, 2).transpose(0, 3, 1, 2, 4).reshape(2, 128, 2 * T), k_scales, "e2m1")
    kg = pick(k, idx)
    c = unpack_weight(c_words.reshape(1, 128, T, 2, 2).transpose(0, 3, 1, 2, 4).reshape(2, 128, 2 * T), c_scales, "e2m1")
    cg = pick(c, idx)
    hiq = mxq(np.maximum(f64(qT), 0.0), 1, "e4m3")
    loq = mxq(np.minimum(f64(qT), 0.0), 1, "e4m3")
    a = (hiq.transpose(0, 2, 1) @ kg) + (loq.transpose(0, 2, 1) @ cg)
    y = a - f64(th)
    out = np.zeros((B, NQ, T))
    for b in range(B):
        out[b][:, idx[b * N:(b + 1) * N]] = y[b]
    return out

@@ -1,0 +1,126 @@
+from contextlib import ExitStack
+
+import concourse.mybir as mybir
+
+P, N, T, D, NQ = 128, 512, 2048, 1024, 128
+PACK = 4
+PASSES = D // (P * PACK)
+HALF = N // 2
+FLOPS = 2 * 2 * D * NQ * N
+
+F32 = mybir.dt.float32
+BF16 = mybir.dt.bfloat16
+I32 = mybir.dt.int32
+U32 = mybir.dt.uint32
+U16 = mybir.dt.uint16
+U8 = mybir.dt.uint8
+FP8X4 = mybir.dt.float8_e4m3fn_x4
+FP4X4 = mybir.dt.float4_e2m1fn_x4
+ACT = mybir.ActivationFunctionType
+ALU = mybir.AluOpType
+
+
+def tile_attend_questscat_topk_kernel(tc, qT, k_words, k_scales, c_words, c_scales, th, offs, out):
+    nc = tc.nc
+    with ExitStack() as ctx:
+        pool = ctx.enter_context(tc.tile_pool(name="held", bufs=1))
+        psum = ctx.enter_context(tc.psum_pool(name="psum", bufs=1))
+
+        offsets = pool.tile([P, N // 16], U16, name="offsets")
+        nc.sync.dma_start(offsets[:], offs)
+
+        tables = (("k", k_words, k_scales, 96), ("c", c_words, c_scales, 0))
+        scale_win, word_win = {}, {}
+        for name, words, scales, base in tables:
+            win = pool.tile([P, T], U8, name=name + "_scale_win", align_bytes=64)
+            nc.sync.dma_start(win[base:base + 32, :].bitcast(I32), scales.rearrange("o f t -> f o t").bitcast(I32))
+            for lo, hi in ((32, 64), (64, 128)) if base == 0 else ((0, 96),):
+                nc.vector.memset(win[lo:hi, :].bitcast(I32), 0)
+            scale_win[name] = win
+
+        word_win["k"] = pool.tile([P, T], U32, name="k_word_win", align_bytes=64)
+        nc.sync.dma_start(word_win["k"][:].bitcast(I32), k_words[0].rearrange("p t b -> p (t b)").bitcast(I32))
+        q_raw = pool.tile([P, PASSES, PACK, NQ], F32, name="q_raw")
+        nc.sync.dma_start(q_raw[:], qT[0].rearrange("(o p j) n -> p o j n", o=PASSES, j=PACK))
+        word_win["c"] = pool.tile([P, T], U32, name="c_word_win", align_bytes=64)
+        nc.sync.dma_start(word_win["c"][:].bitcast(I32), c_words[0].rearrange("p t b -> p (t b)").bitcast(I32))
+
+        th_col = pool.tile([P, 1], F32, name="th_col")
+        nc.scalar.dma_start(th_col[:], th[0])
+        neg_th = pool.tile([P, 1], F32, name="neg_th")
+        nc.scalar.activation(neg_th[:], th_col[:], ACT.Identity, scale=-1.0)
+
+        planes = {}
+        for name, words, scales, base in tables:
+            planes[name] = pool.tile([P, PASSES * N], U8, name=name + "_planes", align_bytes=64)
+            nc.vector.memset(planes[name][:].bitcast(I32), 0)
+        result = pool.tile([P, T], F32, name="result")
+        nc.vector.memset(result[:], 0.0)
+
+        for name, words, scales, base in tables:
+            picked = pool.tile([P, N], U8, name=name + "_scale_picked", align_bytes=64)
+            nc.vector.tensor_copy(picked[:], scale_win[name][:].indirect(offsets[:]))
+            queue = nc.scalar if name == "k" else nc.sync
+            for quad in range(4):
+                queue.dma_start(
+                    planes[name][32 * quad:32 * quad + 4, :].bitcast(I32),
+                    picked[base + 8 * quad:base + 8 * quad + 8, :].bitcast(I32),
+                )
+
+        def gather_words(name, first, count):
+            tag = name + str(first)
+            pairs = pool.tile([P, count], U32, name=tag + "_pairs", align_bytes=64)
+            nc.vector.tensor_copy(pairs[:], word_win[name][:].indirect(offsets[:, first // 16:(first + count) // 16]))
+            parted = pool.tile([P, PASSES, count], U16, name=tag + "_parted", align_bytes=64)
+            nc.vector.tensor_copy(parted[:], pairs[:].bitcast(U16).rearrange("p (i o) -> p o i", o=PASSES))
+            return parted
+
+        def product(name, acc, parted, first, cols):
+            for o in range(PASSES):
+                nc.tensor.matmul_mx(
+                    out=acc[:, cols],
+                    lhsT=codes[name][:, o * NQ:(o + 1) * NQ].bitcast(FP8X4),
+                    lhsT_scale=q_scales[name][:, o * NQ:(o + 1) * NQ],
+                    rhs=parted[:, o, cols].bitcast(FP4X4),
+                    rhs_scale=planes[name][:, o * N + first + cols.start:o * N + first + cols.stop],
+                    start=(o == 0),
+                    stop=(o == PASSES - 1),
+                )
+
+        k_parted = gather_words("k", 0, N)
+
+        q_view = q_raw[:].rearrange("p o j n -> p o n j")
+        hi = pool.tile([P, PASSES, NQ, PACK], BF16, name="hi", align_bytes=64)
+        nc.scalar.activation(hi[:], q_view, ACT.Relu)
+        lo = pool.tile([P, PASSES, NQ, PACK], BF16, name="lo", align_bytes=64)
+        nc.vector.tensor_scalar(lo[:], q_view, 0.0, None, ALU.min)
+        codes, q_scales = {}, {}
+        for name, part in (("k", hi), ("c", lo)):
+            codes[name] = pool.tile([P, PASSES * NQ], U32, name=name + "_q_codes", align_bytes=64)
+            q_scales[name] = pool.tile([P, PASSES * NQ], U8, name=name + "_q_scales", align_bytes=64)
+            nc.vector.quantize_mx(
+                out=codes[name][:].bitcast(FP8X4),
+                scales=q_scales[name][:],
+                in_=part[:].rearrange("p o n j -> p (o n j)"),
+            )
+
+        k_acc = psum.tile([NQ, N], F32, name="k_acc")
+        product("k", k_acc, k_parted, 0, slice(0, N))
+        k_less_th = pool.tile([NQ, N], F32, name="k_less_th")
+        nc.scalar.activation(k_less_th[:], k_acc[:], ACT.Identity, bias=neg_th[:])
+
+        c_sums = []
+        for first in range(0, N, HALF):
+            c_parted = gather_words("c", first, HALF)
+            c_acc = psum.tile([NQ, HALF], F32, name="c_acc" + str(first))
+            for col in range(0, HALF, P):
+                product("c", c_acc, c_parted, first, slice(col, col + P))
+            c_sum = pool.tile([NQ, HALF], F32, name="c_sum" + str(first))
+            nc.scalar.copy(c_sum[:], c_acc[:])
+            c_sums.append(c_sum)
+        for first, c_sum in zip(range(0, N, HALF), c_sums):
+            nc.vector.tensor_tensor(
+                result[:].indirect(offsets[:, first // 16:(first + HALF) // 16]),
+                k_less_th[:, first:first + HALF], c_sum[:], ALU.add,
+            )
+        nc.sync.dma_start(out[0], result[:])

@@ -29,47 +29,40 @@ def tile_attend_questscat_topk_kernel(tc, qT, k_words, k_scales, c_words, c_scal
         offsets = pool.tile([P, N // 16], U16, name="offsets")
         nc.sync.dma_start(offsets[:], offs)
 
-        tables = (("k", k_words, k_scales, 96), ("c", c_words, c_scales, 0))
+        base = 96
         scale_win, word_win = {}, {}
-        for name, words, scales, base in tables:
-            win = pool.tile([P, T], U8, name=name + "_scale_win", align_bytes=64)
-            nc.sync.dma_start(win[base:base + 32, :].bitcast(I32), scales.rearrange("o f t -> f o t").bitcast(I32))
-            for lo, hi in ((32, 64), (64, 128)) if base == 0 else ((0, 96),):
-                nc.vector.memset(win[lo:hi, :].bitcast(I32), 0)
+        for name, scales in (("k", k_scales), ("c", c_scales)):
+            win = pool.tile([P, T + 4], U8, name=name + "_scale_win", align_bytes=64)
+            (nc.scalar if name == "k" else nc.sync).dma_start(win[base:, :T].bitcast(I32), scales.rearrange("o f t -> f o t").bitcast(I32))
+            nc.vector.memset(win[:base, :].bitcast(I32), 0)
             scale_win[name] = win
 
-        word_win["k"] = pool.tile([P, T], U32, name="k_word_win", align_bytes=64)
-        nc.sync.dma_start(word_win["k"][:].bitcast(I32), k_words[0].rearrange("p t b -> p (t b)").bitcast(I32))
         q_raw = pool.tile([P, PASSES, PACK, NQ], F32, name="q_raw")
         nc.sync.dma_start(q_raw[:], qT[0].rearrange("(o p j) n -> p o j n", o=PASSES, j=PACK))
+        word_win["k"] = pool.tile([P, T], U32, name="k_word_win", align_bytes=64)
+        nc.sync.dma_start(word_win["k"][:].bitcast(I32), k_words[0].rearrange("p t b -> p (t b)").bitcast(I32))
+        th_col = pool.tile([P, 1], F32, name="th_col")
+        nc.scalar.dma_start(th_col[:], th[0])
         word_win["c"] = pool.tile([P, T], U32, name="c_word_win", align_bytes=64)
         nc.sync.dma_start(word_win["c"][:].bitcast(I32), c_words[0].rearrange("p t b -> p (t b)").bitcast(I32))
 
-        th_col = pool.tile([P, 1], F32, name="th_col")
-        nc.scalar.dma_start(th_col[:], th[0])
-        neg_th = pool.tile([P, 1], F32, name="neg_th")
-        nc.scalar.activation(neg_th[:], th_col[:], ACT.Identity, scale=-1.0)
-
-        planes = {}
-        for name, words, scales, base in tables:
-            planes[name] = pool.tile([P, PASSES * N], U8, name=name + "_planes", align_bytes=64)
-            nc.vector.memset(planes[name][:].bitcast(I32), 0)
+        planes = pool.tile([P, PASSES * 2 * N + 4], U8, name="planes", align_bytes=64)
+        nc.vector.memset(planes[:].bitcast(I32), 0)
         result = pool.tile([P, T], F32, name="result")
-        nc.vector.memset(result[:], 0.0)
+        nc.gpsimd.memset(result[:], 0.0)
 
-        for name, words, scales, base in tables:
-            picked = pool.tile([P, N], U8, name=name + "_scale_picked", align_bytes=64)
-            nc.vector.tensor_copy(picked[:], scale_win[name][:].indirect(offsets[:]))
-            queue = nc.scalar if name == "k" else nc.sync
-            for quad in range(4):
-                queue.dma_start(
-                    planes[name][32 * quad:32 * quad + 4, :].bitcast(I32),
-                    picked[base + 8 * quad:base + 8 * quad + 8, :].bitcast(I32),
-                )
+        picked = pool.tile([P, 2 * N], U8, name="scale_picked", align_bytes=64)
+        for slot, name in enumerate("kc"):
+            nc.vector.tensor_copy(picked[:, slot * N:(slot + 1) * N], scale_win[name][:, :T].indirect(offsets[:]))
+        for quad in range(4):
+            nc.sync.dma_start(
+                planes[32 * quad:32 * quad + 4, :PASSES * 2 * N].bitcast(I32),
+                picked[base + 8 * quad:base + 8 * quad + 8, :].bitcast(I32),
+            )
 
         def gather_words(name, first, count):
             tag = name + str(first)
-            pairs = pool.tile([P, count], U32, name=tag + "_pairs", align_bytes=64)
+            pairs = pool.tile([P, count], U32, name=tag + "_pairs", tag=name + "_pairs", align_bytes=64)
             nc.vector.tensor_copy(pairs[:], word_win[name][:].indirect(offsets[:, first // 16:(first + count) // 16]))
             parted = pool.tile([P, PASSES, count], U16, name=tag + "_parted", align_bytes=64)
             nc.vector.tensor_copy(parted[:], pairs[:].bitcast(U16).rearrange("p (i o) -> p o i", o=PASSES))
@@ -77,21 +70,22 @@ def tile_attend_questscat_topk_kernel(tc, qT, k_words, k_scales, c_words, c_scal
 
         def product(name, acc, parted, first, cols):
             for o in range(PASSES):
+                plane = (2 * o + "kc".index(name)) * N + first
                 nc.tensor.matmul_mx(
                     out=acc[:, cols],
                     lhsT=codes[name][:, o * NQ:(o + 1) * NQ].bitcast(FP8X4),
                     lhsT_scale=q_scales[name][:, o * NQ:(o + 1) * NQ],
                     rhs=parted[:, o, cols].bitcast(FP4X4),
-                    rhs_scale=planes[name][:, o * N + first + cols.start:o * N + first + cols.stop],
+                    rhs_scale=planes[:, plane + cols.start:plane + cols.stop],
                     start=(o == 0),
                     stop=(o == PASSES - 1),
                 )
 
-        k_parted = gather_words("k", 0, N)
-
         q_view = q_raw[:].rearrange("p o j n -> p o n j")
         hi = pool.tile([P, PASSES, NQ, PACK], BF16, name="hi", align_bytes=64)
         nc.scalar.activation(hi[:], q_view, ACT.Relu)
+        neg_th = pool.tile([P, 1], F32, name="neg_th")
+        nc.scalar.activation(neg_th[:], th_col[:], ACT.Identity, scale=-1.0)
         lo = pool.tile([P, PASSES, NQ, PACK], BF16, name="lo", align_bytes=64)
         nc.vector.tensor_scalar(lo[:], q_view, 0.0, None, ALU.min)
         codes, q_scales = {}, {}
@@ -104,6 +98,7 @@ def tile_attend_questscat_topk_kernel(tc, qT, k_words, k_scales, c_words, c_scal
                 in_=part[:].rearrange("p o n j -> p (o n j)"),
             )
 
+        k_parted = gather_words("k", 0, N)
         k_acc = psum.tile([NQ, N], F32, name="k_acc")
         product("k", k_acc, k_parted, 0, slice(0, N))
         k_less_th = pool.tile([NQ, N], F32, name="k_less_th")

@@ -60,25 +60,26 @@ def tile_attend_questscat_topk_kernel(tc, qT, k_words, k_scales, c_words, c_scal
                 picked[base + 8 * quad:base + 8 * quad + 8, :].bitcast(I32),
             )
 
-        def gather_words(name, first, count):
-            tag = name + str(first)
-            pairs = pool.tile([P, count], U32, name=tag + "_pairs", tag=name + "_pairs", align_bytes=64)
-            nc.vector.tensor_copy(pairs[:], word_win[name][:].indirect(offsets[:, first // 16:(first + count) // 16]))
-            parted = pool.tile([P, PASSES, count], U16, name=tag + "_parted", align_bytes=64)
-            nc.vector.tensor_copy(parted[:], pairs[:].bitcast(U16).rearrange("p (i o) -> p o i", o=PASSES))
+        def gather_words(name, pairs, first, count, extra):
+            nc.vector.tensor_copy(
+                pairs[:, first:first + count + extra],
+                word_win[name][:].indirect(offsets[:, first // 16:(first + count + extra) // 16]),
+            )
+            parted = pool.tile([P, PASSES, count], U16, name=name + str(first) + "_parted", align_bytes=64)
+            nc.vector.tensor_copy(parted[:], pairs[:, first:first + count].bitcast(U16).rearrange("p (i o) -> p o i", o=PASSES))
             return parted
 
-        def product(name, acc, parted, first, cols):
+        def product(name, parted, first, col):
             for o in range(PASSES):
-                plane = (2 * o + "kc".index(name)) * N + first
+                plane = (2 * o + "kc".index(name)) * N + col
                 nc.tensor.matmul_mx(
-                    out=acc[:, cols],
+                    out=banks[col // P][:],
                     lhsT=codes[name][:, o * NQ:(o + 1) * NQ].bitcast(FP8X4),
                     lhsT_scale=q_scales[name][:, o * NQ:(o + 1) * NQ],
-                    rhs=parted[:, o, cols].bitcast(FP4X4),
-                    rhs_scale=planes[:, plane + cols.start:plane + cols.stop],
-                    start=(o == 0),
-                    stop=(o == PASSES - 1),
+                    rhs=parted[:, o, col - first:col - first + P].bitcast(FP4X4),
+                    rhs_scale=planes[:, plane:plane + P],
+                    start=(name == "k" and o == 0),
+                    stop=(name == "c" and o == PASSES - 1),
                 )
 
         q_view = q_raw[:].rearrange("p o j n -> p o n j")
@@ -98,24 +99,22 @@ def tile_attend_questscat_topk_kernel(tc, qT, k_words, k_scales, c_words, c_scal
                 in_=part[:].rearrange("p o n j -> p (o n j)"),
             )
 
-        k_parted = gather_words("k", 0, N)
-        k_acc = psum.tile([NQ, N], F32, name="k_acc")
-        product("k", k_acc, k_parted, 0, slice(0, N))
-        k_less_th = pool.tile([NQ, N], F32, name="k_less_th")
-        nc.scalar.activation(k_less_th[:], k_acc[:], ACT.Identity, bias=neg_th[:])
+        k_pairs = pool.tile([P, N], U32, name="k_pairs", align_bytes=64)
+        k_parted = gather_words("k", k_pairs, 0, N, 0)
+        banks = [psum.tile([NQ, P], F32, name="bank" + str(g)) for g in range(N // P)]
+        for col in range(0, N, P):
+            product("k", k_parted, 0, col)
 
-        c_sums = []
+        y = pool.tile([NQ, N], F32, name="y")
+        c_pairs = pool.tile([P, N], U32, name="c_pairs", align_bytes=64)
         for first in range(0, N, HALF):
-            c_parted = gather_words("c", first, HALF)
-            c_acc = psum.tile([NQ, HALF], F32, name="c_acc" + str(first))
-            for col in range(0, HALF, P):
-                product("c", c_acc, c_parted, first, slice(col, col + P))
-            c_sum = pool.tile([NQ, HALF], F32, name="c_sum" + str(first))
-            nc.scalar.copy(c_sum[:], c_acc[:])
-            c_sums.append(c_sum)
-        for first, c_sum in zip(range(0, N, HALF), c_sums):
-            nc.vector.tensor_tensor(
-                result[:].indirect(offsets[:, first // 16:(first + HALF) // 16]),
-                k_less_th[:, first:first + HALF], c_sum[:], ALU.add,
+            c_parted = gather_words("c", c_pairs, first, HALF, 16 if first == 0 else 0)
+            for col in range(first, first + HALF, P):
+                product("c", c_parted, first, col)
+                nc.scalar.activation(y[:, col:col + P], banks[col // P][:], ACT.Identity, bias=neg_th[:])
+        for first in range(0, N, HALF):
+            nc.vector.tensor_copy(
+                result[:].indirect(offsets[:, first // 16:(first + HALF) // 16]), y[:, first:first + HALF]
             )
-        nc.sync.dma_start(out[0], result[:])
+        nc.sync.dma_start(out[0][:, :T // 2], result[:, :T // 2])
+        nc.scalar.dma_start(out[0][:, T // 2:], result[:, T // 2:])

from contextlib import ExitStack

import concourse.mybir as mybir

P, N, T, D, NQ = 128, 512, 2048, 1024, 128
PACK = 4
PASSES = D // (P * PACK)
HALF = N // 2
FLOPS = 2 * 2 * D * NQ * N

F32 = mybir.dt.float32
BF16 = mybir.dt.bfloat16
I32 = mybir.dt.int32
U32 = mybir.dt.uint32
U16 = mybir.dt.uint16
U8 = mybir.dt.uint8
FP8X4 = mybir.dt.float8_e4m3fn_x4
FP4X4 = mybir.dt.float4_e2m1fn_x4
ACT = mybir.ActivationFunctionType
ALU = mybir.AluOpType


def tile_attend_questscat_topk_kernel(tc, qT, k_words, k_scales, c_words, c_scales, th, offs, out):
    nc = tc.nc
    with ExitStack() as ctx:
        pool = ctx.enter_context(tc.tile_pool(name="held", bufs=1))
        psum = ctx.enter_context(tc.psum_pool(name="psum", bufs=1))

        offsets = pool.tile([P, N // 16], U16, name="offsets")
        nc.sync.dma_start(offsets[:], offs)

        base = 96
        scale_win, word_win = {}, {}
        for name, scales in (("k", k_scales), ("c", c_scales)):
            win = pool.tile([P, T + 4], U8, name=name + "_scale_win", align_bytes=64)
            (nc.scalar if name == "k" else nc.sync).dma_start(win[base:, :T].bitcast(I32), scales.rearrange("o f t -> f o t").bitcast(I32))
            nc.vector.memset(win[:base, :].bitcast(I32), 0)
            scale_win[name] = win

        q_raw = pool.tile([P, PASSES, PACK, NQ], F32, name="q_raw")
        nc.sync.dma_start(q_raw[:], qT[0].rearrange("(o p j) n -> p o j n", o=PASSES, j=PACK))
        word_win["k"] = pool.tile([P, T], U32, name="k_word_win", align_bytes=64)
        nc.sync.dma_start(word_win["k"][:].bitcast(I32), k_words[0].rearrange("p t b -> p (t b)").bitcast(I32))
        th_col = pool.tile([P, 1], F32, name="th_col")
        nc.scalar.dma_start(th_col[:], th[0])
        word_win["c"] = pool.tile([P, T], U32, name="c_word_win", align_bytes=64)
        nc.sync.dma_start(word_win["c"][:].bitcast(I32), c_words[0].rearrange("p t b -> p (t b)").bitcast(I32))

        planes = pool.tile([P, PASSES * 2 * N + 4], U8, name="planes", align_bytes=64)
        nc.vector.memset(planes[:].bitcast(I32), 0)
        result = pool.tile([P, T], F32, name="result")
        nc.gpsimd.memset(result[:], 0.0)

        picked = pool.tile([P, 2 * N], U8, name="scale_picked", align_bytes=64)
        for slot, name in enumerate("kc"):
            nc.vector.tensor_copy(picked[:, slot * N:(slot + 1) * N], scale_win[name][:, :T].indirect(offsets[:]))
        for quad in range(4):
            nc.sync.dma_start(
                planes[32 * quad:32 * quad + 4, :PASSES * 2 * N].bitcast(I32),
                picked[base + 8 * quad:base + 8 * quad + 8, :].bitcast(I32),
            )

        def gather_words(name, pairs, first, count, extra):
            nc.vector.tensor_copy(
                pairs[:, first:first + count + extra],
                word_win[name][:].indirect(offsets[:, first // 16:(first + count + extra) // 16]),
            )
            parted = pool.tile([P, PASSES, count], U16, name=name + str(first) + "_parted", align_bytes=64)
            nc.vector.tensor_copy(parted[:], pairs[:, first:first + count].bitcast(U16).rearrange("p (i o) -> p o i", o=PASSES))
            return parted

        def product(name, parted, first, col):
            for o in range(PASSES):
                plane = (2 * o + "kc".index(name)) * N + col
                nc.tensor.matmul_mx(
                    out=banks[col // P][:],
                    lhsT=codes[name][:, o * NQ:(o + 1) * NQ].bitcast(FP8X4),
                    lhsT_scale=q_scales[name][:, o * NQ:(o + 1) * NQ],
                    rhs=parted[:, o, col - first:col - first + P].bitcast(FP4X4),
                    rhs_scale=planes[:, plane:plane + P],
                    start=(name == "k" and o == 0),
                    stop=(name == "c" and o == PASSES - 1),
                )

        q_view = q_raw[:].rearrange("p o j n -> p o n j")
        hi = pool.tile([P, PASSES, NQ, PACK], BF16, name="hi", align_bytes=64)
        nc.scalar.activation(hi[:], q_view, ACT.Relu)
        neg_th = pool.tile([P, 1], F32, name="neg_th")
        nc.scalar.activation(neg_th[:], th_col[:], ACT.Identity, scale=-1.0)
        lo = pool.tile([P, PASSES, NQ, PACK], BF16, name="lo", align_bytes=64)
        nc.vector.tensor_scalar(lo[:], q_view, 0.0, None, ALU.min)
        codes, q_scales = {}, {}
        for name, part in (("k", hi), ("c", lo)):
            codes[name] = pool.tile([P, PASSES * NQ], U32, name=name + "_q_codes", align_bytes=64)
            q_scales[name] = pool.tile([P, PASSES * NQ], U8, name=name + "_q_scales", align_bytes=64)
            nc.vector.quantize_mx(
                out=codes[name][:].bitcast(FP8X4),
                scales=q_scales[name][:],
                in_=part[:].rearrange("p o n j -> p (o n j)"),
            )

        k_pairs = pool.tile([P, N], U32, name="k_pairs", align_bytes=64)
        k_parted = gather_words("k", k_pairs, 0, N, 0)
        banks = [psum.tile([NQ, P], F32, name="bank" + str(g)) for g in range(N // P)]
        for col in range(0, N, P):
            product("k", k_parted, 0, col)

        y = pool.tile([NQ, N], F32, name="y")
        c_pairs = pool.tile([P, N], U32, name="c_pairs", align_bytes=64)
        for first in range(0, N, HALF):
            c_parted = gather_words("c", c_pairs, first, HALF, 16 if first == 0 else 0)
            for col in range(first, first + HALF, P):
                product("c", c_parted, first, col)
                nc.scalar.activation(y[:, col:col + P], banks[col // P][:], ACT.Identity, bias=neg_th[:])
        for first in range(0, N, HALF):
            nc.vector.tensor_copy(
                result[:].indirect(offsets[:, first // 16:(first + HALF) // 16]), y[:, first:first + HALF]
            )
        nc.sync.dma_start(out[0][:, :T // 2], result[:, :T // 2])
        nc.scalar.dma_start(out[0][:, T // 2:], result[:, T // 2:])
